import numpy as np
import ml_dtypes


def mxq(x, axis, fmt="e4m3"):
    dtype, down = {"e4m3": (ml_dtypes.float8_e4m3fn, 7), "e5m2": (ml_dtypes.float8_e5m2, 14)}[fmt]
    v = np.moveaxis(np.asarray(x, np.float32).astype(ml_dtypes.bfloat16).astype(np.float64), axis, -1)
    blocks = v.reshape(v.shape[:-1] + (-1, 32))
    amax = np.abs(blocks).max(-1, keepdims=True)
    byte = np.maximum(np.where(amax > 0, np.frexp(amax)[1] - 1 + 127, 0) - down, 1)
    scale = np.exp2(byte - 127.0)
    codes = (blocks / scale).astype(np.float32).astype(dtype).astype(np.float64)
    return np.moveaxis((codes * scale).reshape(v.shape), -1, axis)


WIDE = False


def mx_kscale(k):
    if not WIDE:
        return np.ones(k)
    levels = np.array([10, -10, 5, -5, 0])
    if k % 512:
        return np.exp2(np.random.permutation(np.resize(levels, k // 32))).repeat(32)
    a = np.empty((k // 512, 16))
    for p in range(k // 512):
        a[p, :8] = np.random.permutation(np.resize(levels, 8))
        for g in range(8):
            far = levels[np.abs(levels - a[p, g]) >= 10]
            a[p, g + 8] = far[np.random.randint(len(far))]
    return np.exp2(a.ravel()).repeat(32)


def f64(x):
    return np.asarray(x).astype(np.float64)


def striped(idx):
    return np.tile(idx.reshape(-1, 16).T, (8, 1)).astype(np.uint16)


def unstriped(offs):
    return offs[:16].T.reshape(-1).astype(np.int64)


E2M1 = np.array([0.0, 0.5, 1.0, 1.5, 2.0, 3.0, 4.0, 6.0, -0.0, -0.5, -1.0, -1.5, -2.0, -3.0, -4.0, -6.0])


def pack_weight(w, fmt):
    k, n = w.shape
    w = f64(np.asarray(w, np.float32).astype(ml_dtypes.bfloat16)).reshape(k // 32, 32, n)
    amax = np.abs(w).max(1)
    if fmt == "e4m3":
        byte = np.frexp(amax)[1] - 1 + 127 - 7
    else:
        mant, ex = np.frexp(amax / 6.0)
        byte = np.where(mant > 0.5, ex, ex - 1) + 127
    byte = np.clip(np.where(amax > 0, byte, 1), 1, 254)
    scaled = (w * np.exp2(127.0 - byte)[:, None, :]).reshape(k, n).astype(np.float32)
    by_word = np.ascontiguousarray(scaled.reshape(k // 512, 128, 4, n).transpose(0, 1, 3, 2))
    if fmt == "e4m3":
        words = by_word.astype(ml_dtypes.float8_e4m3fn).view(np.uint8)
    else:
        c = by_word.astype(ml_dtypes.float4_e2m1fn).view(np.uint8) & 0xF
        words = (c[..., 0::2] | (c[..., 1::2] << 4)).reshape(k // 512, 128, 2 * n)
    return np.ascontiguousarray(words), np.ascontiguousarray(byte.astype(np.uint8).reshape(k // 512, 16, n))


def unpack_weight(words, scales, fmt):
    g, _, n = scales.shape
    words = np.ascontiguousarray(words).reshape(g, 128, n, -1)
    if fmt == "e4m3":
        vals = words.view(ml_dtypes.float8_e4m3fn).astype(np.float64)
    else:
        nib = np.empty((g, 128, n, 4), np.uint8)
        nib[..., 0::2] = words & 0xF
        nib[..., 1::2] = words >> 4
        vals = E2M1[nib]
    vals = vals * np.repeat(np.exp2(scales.astype(np.float64) - 127.0), 8, axis=1)[..., None]
    return vals.transpose(0, 1, 3, 2).reshape(g * 512, n)


def gelu(v):
    return 0.5 * v * (1.0 + np.tanh(np.sqrt(2.0 / np.pi) * (v + 0.044715 * v**3)))


K1, K2, H, T, S, T2, P, R = 1024, 512, 1024, 2048, 512, 2048, 1024, 128

def setup_inputs():
    n = np.random.standard_normal
    s, s2, u = mx_kscale(K1)[:, None], mx_kscale(K2)[:, None], mx_kscale(H)[:, None]
    d = {}
    d["tab_words"], d["tab_scales"] = pack_weight(n((K1, T)) * s, "e4m3")
    d["tab2_words"], d["tab2_scales"] = pack_weight(n((K2, T)) * s2, "e4m3")
    d["offs"] = striped(np.random.permutation(T)[:S])
    d["offs2"] = striped(np.random.permutation(T)[:S])
    perm = np.random.permutation(T2)
    d["offs3"] = striped(perm[:S])
    d["offs4"] = striped(perm[S:2 * S])
    d["offs5"] = striped(np.random.permutation(T2)[:P])
    d["wa"] = (n((K1, H)) / s * u.T / K1 ** 0.5).astype(np.float32)
    d["wf_words"], d["wf_scales"] = pack_weight(1.5 * n((K2, H)) / s2 / K2 ** 0.5, "e2m1")
    d["gf"] = (np.exp(0.3 * n(H)) * u[:, 0]).astype(np.float32)
    d["page0"] = (n((H, T2)) * u).astype(np.float32)
    d["wg1"] = np.exp(0.3 * n((R, S))).astype(np.float32)
    d["wg2"] = np.exp(0.3 * n((R, S))).astype(np.float32)
    d["ex"] = np.exp(0.5 * n((H, P))).astype(np.float32)
    d["ws"] = (n((H, H)) / u / u.T / H ** 0.5).astype(np.float32)
    d["wr_words"], d["wr_scales"] = pack_weight(n((H, H)) / u / H ** 0.5, "e4m3")
    return d

def reference(tab_words, tab_scales, tab2_words, tab2_scales, offs, offs2, offs3, offs4, offs5, wa, wf_words, wf_scales, gf, page0, wg1, wg2, ex, ws, wr_words, wr_scales):
    v = unpack_weight(tab_words, tab_scales, "e4m3")[:, unstriped(offs)]
    v2 = unpack_weight(tab2_words, tab2_scales, "e4m3")[:, unstriped(offs2)]
    h1 = np.abs(mxq(f64(wa), 0, "e4m3").T @ v)
    b = unpack_weight(wf_words, wf_scales, "e2m1").T @ v2
    h2 = 0.5 * b * (1.0 + np.tanh(0.7978845608 * (b + 0.044715 * b ** 3))) * f64(gf)[:, None]
    page = f64(page0).copy()
    page[:, unstriped(offs3)] = np.tile(f64(wg1), (H // R, 1)) * h1
    page[:, unstriped(offs4)] = np.tile(f64(wg2), (H // R, 1)) * h2
    x = page[:, unstriped(offs5)]
    z = mxq(x * f64(ex), 0, "e4m3")
    y = mxq(f64(ws), 0, "e4m3").T @ z
    rest = unpack_weight(wr_words, wr_scales, "e4m3").T @ z
    return y * x + rest

@@ -1,0 +1,292 @@
+from contextlib import ExitStack
+
+import concourse.mybir as mybir
+
+K1, K2, H, T, S, T2, M = 1024, 512, 1024, 2048, 512, 2048, 1024
+FLOPS = 2 * (K1 * H * S + K2 * H * S + 2 * H * H * M)
+
+F32 = mybir.dt.float32
+BF16 = mybir.dt.bfloat16
+I32 = mybir.dt.int32
+U32 = mybir.dt.uint32
+U16 = mybir.dt.uint16
+U8 = mybir.dt.uint8
+FP8X4 = mybir.dt.float8_e4m3fn_x4
+FP4X4 = mybir.dt.float4_e2m1fn_x4
+MULT = mybir.AluOpType.mult
+ADD = mybir.AluOpType.add
+ACT = mybir.ActivationFunctionType
+
+P = 128
+PACK = 4
+KP = P * PACK
+NB = 512
+
+
+def tile_list_deicing_slot_scores_kernel(
+    tc, tab_words, tab_scales, tab2_words, tab2_scales, offs, offs2, offs3, offs4, offs5,
+    wa, wf_words, wf_scales, gf, page0, wg1, wg2, ex, ws, wr_words, wr_scales, out,
+):
+    nc = tc.nc
+    with ExitStack() as ctx:
+        lists = ctx.enter_context(tc.tile_pool(name="lists", bufs=1))
+        keep = ctx.enter_context(tc.tile_pool(name="keep", bufs=1))
+        stream = ctx.enter_context(tc.tile_pool(name="stream", bufs=5))
+        woven = ctx.enter_context(tc.tile_pool(name="woven", bufs=3))
+        flat = ctx.enter_context(tc.tile_pool(name="flat", bufs=2))
+        feat = ctx.enter_context(tc.tile_pool(name="feat", bufs=4))
+        psum = ctx.enter_context(tc.psum_pool(name="psum", bufs=8))
+
+        def load_list(src, name):
+            t = lists.tile(list(src.shape), U16, name=name)
+            nc.sync.dma_start(t[:], src)
+            return t
+
+        def zeroed_plane(width, name):
+            t = keep.tile([P, width], U8, name=name, align_bytes=64)
+            nc.vector.memset(t[:].bitcast(I32), 0)
+            return t
+
+        def load_scale_rows(plane, src):
+            passes = src.shape[0]
+            for q in range(4):
+                nc.sync.dma_start(
+                    out=plane[32 * q : 32 * q + 4 * passes, :].bitcast(I32),
+                    in_=src[:, 4 * q : 4 * q + 4, :].bitcast(I32),
+                )
+
+        def load_table_words(src, name):
+            t = stream.tile([P, T], U32, name=name, tag="big", align_bytes=64)
+            nc.sync.dma_start(out=t[:].bitcast(I32), in_=src.rearrange("p t i -> p (t i)").bitcast(I32))
+            return t
+
+        def gather(window, offsets, dtype, name):
+            t = keep.tile([P, S], dtype, name=name, align_bytes=64)
+            nc.vector.tensor_copy(t[:], window[:].indirect(offsets[:]))
+            return t
+
+        def load_rows(src, g, c, name):
+            t = stream.tile([P, PACK, NB], F32, name=name, tag="big", align_bytes=64)
+            nc.sync.dma_start(
+                out=t[:],
+                in_=src[KP * g : KP * (g + 1), NB * c : NB * (c + 1)].rearrange("(p j) c -> p j c", j=PACK),
+            )
+            return t
+
+        def quantise(src, name, tag):
+            codes = keep.tile([P, NB], U32, name=name + "c", tag=tag + "c", align_bytes=64)
+            scales = keep.tile([P, NB], U8, name=name + "s", tag=tag + "s", align_bytes=64)
+            nc.vector.quantize_mx(out=codes[:].bitcast(FP8X4), scales=scales[:], in_=src[:])
+            return codes, scales
+
+        def quantise_weight(raw, name, tag):
+            w = woven.tile([P, PACK * NB], BF16, name="w", tag="woven", align_bytes=64)
+            nc.scalar.copy(
+                out=w[:].rearrange("p (t m j) -> p m t j", t=PACK, j=PACK),
+                in_=raw[:].rearrange("p j (m t) -> p m t j", t=PACK),
+            )
+            return quantise(w, name, tag)
+
+        def load_page(a, t):
+            pg = keep.tile([P, T2], F32, name="page%d%d" % (a, t), align_bytes=64)
+            nc.sync.dma_start(out=pg[:], in_=page0.rearrange("(a p t) c -> a t p c", a=2, t=PACK)[a, t])
+            return pg
+
+        def load_gain(src, name):
+            t = keep.tile([P, PACK, S], F32, name=name)
+            for q in range(4):
+                nc.sync.dma_start(
+                    out=t[32 * q : 32 * (q + 1), :, :], in_=src.rearrange("(q t) j -> q t j", t=PACK)
+                )
+            return t
+
+        tab2_plane = zeroed_plane(T, "tab2_plane")
+        wf_plane = zeroed_plane(H, "wf_plane")
+        tab_plane = zeroed_plane(T, "tab_plane")
+        wr_plane = zeroed_plane(H, "wr_plane")
+
+        idx2 = load_list(offs2, "idx2")
+        wf_raw = keep.tile([P, 2 * H], U8, name="wf_raw", align_bytes=64)
+        nc.sync.dma_start(out=wf_raw[:].bitcast(I32), in_=wf_words[0].bitcast(I32))
+        tab2_w = load_table_words(tab2_words[0], "tab2_w")
+        load_scale_rows(wf_plane, wf_scales)
+        load_scale_rows(tab2_plane, tab2_scales)
+        idx4 = load_list(offs4, "idx4")
+        gain = lists.tile([P, 2, PACK], F32, name="gain")
+        nc.sync.dma_start(out=gain[:], in_=gf.rearrange("(a p t) -> p a t", a=2, t=PACK))
+        pages = {}
+        pages[0, 0] = load_page(0, 0)
+        g2 = load_gain(wg2, "g2")
+
+        wf_c, wf_s = [], []
+
+        def deal_wf(a):
+            c = keep.tile([P, 2 * KP], U8, name="wf_c%d" % a, align_bytes=64)
+            s = keep.tile([P, KP], U8, name="wf_s%d" % a, align_bytes=64)
+            nc.vector.tensor_copy(
+                out=c[:].rearrange("p (t m e) -> p m t e", t=PACK, e=2),
+                in_=wf_raw[:, 2 * KP * a : 2 * KP * (a + 1)].rearrange("p (m t e) -> p m t e", t=PACK, e=2),
+            )
+            nc.vector.tensor_copy(
+                out=s[:].rearrange("p (t m) -> p m t", t=PACK),
+                in_=wf_plane[:, KP * a : KP * (a + 1)].rearrange("p (m t) -> p m t", t=PACK),
+            )
+            wf_c.append(c)
+            wf_s.append(s)
+
+        deal_wf(0)
+        v2_c = gather(tab2_w, idx2, U32, "v2_c")
+        v2_s = gather(tab2_plane, idx2, U8, "v2_s")
+        deal_wf(1)
+
+        def frost(a, t):
+            acc = psum.tile([P, NB], F32, name="acc", tag="acc")
+            nc.tensor.matmul_mx(
+                out=acc[:],
+                lhsT=wf_c[a][:, 2 * P * t : 2 * P * (t + 1)].bitcast(FP4X4),
+                lhsT_scale=wf_s[a][:, P * t : P * (t + 1)],
+                rhs=v2_c[:].bitcast(FP8X4),
+                rhs_scale=v2_s[:],
+                start=True,
+                stop=True,
+            )
+            h = feat.tile([P, S], F32, name="h", tag="h")
+            nc.scalar.activation(out=h[:], in_=acc[:], func=ACT.Gelu_apprx_tanh)
+            nc.scalar.activation(out=h[:], in_=h[:], func=ACT.Copy, scale=gain[:, a, t : t + 1])
+            nc.vector.tensor_tensor(pages[a, t][:].indirect(idx4[:]), h[:], g2[:, t, :], MULT)
+
+        v_c, wa_q = [], {}
+        frost(0, 0)
+        pages[0, 1] = load_page(0, 1)
+        frost(0, 1)
+        pages[0, 2] = load_page(0, 2)
+        idx = load_list(offs, "idx")
+        tab_w0 = load_table_words(tab_words[0], "tab_w0")
+        frost(0, 2)
+        pages[0, 3] = load_page(0, 3)
+        tab_w1 = load_table_words(tab_words[1], "tab_w1")
+        load_scale_rows(tab_plane, tab_scales)
+        frost(0, 3)
+        v_c.append(gather(tab_w0, idx, U32, "v_c0"))
+        pages[1, 0] = load_page(1, 0)
+        raw00 = load_rows(wa, 0, 0, "wa00")
+        frost(1, 0)
+        v_c.append(gather(tab_w1, idx, U32, "v_c1"))
+        pages[1, 1] = load_page(1, 1)
+        raw10 = load_rows(wa, 1, 0, "wa10")
+        frost(1, 1)
+        v_s = gather(tab_plane, idx, U8, "v_s")
+        wa_q[0, 0] = quantise_weight(raw00, "wa00", "q00")
+        pages[1, 2] = load_page(1, 2)
+        idx3 = load_list(offs3, "idx3")
+        g1 = load_gain(wg1, "g1")
+        frost(1, 2)
+        wa_q[1, 0] = quantise_weight(raw10, "wa10", "q01")
+        pages[1, 3] = load_page(1, 3)
+        frost(1, 3)
+
+        def weather(a, t):
+            acc = psum.tile([P, NB], F32, name="acc", tag="acc")
+            for g in range(2):
+                codes, scales = wa_q[g, a]
+                nc.tensor.matmul_mx(
+                    out=acc[:],
+                    lhsT=codes[:, P * t : P * (t + 1)].bitcast(FP8X4),
+                    lhsT_scale=scales[:, P * t : P * (t + 1)],
+                    rhs=v_c[g][:].bitcast(FP8X4),
+                    rhs_scale=v_s[4 * g :, :],
+                    start=(g == 0),
+                    stop=(g == 1),
+                )
+            h = feat.tile([P, S], F32, name="h", tag="h")
+            nc.scalar.activation(out=h[:], in_=acc[:], func=ACT.Abs)
+            nc.vector.tensor_tensor(pages[a, t][:].indirect(idx3[:]), h[:], g1[:, t, :], MULT)
+
+        raws = [load_rows(wa, g, 1, "wa%d1" % g) for g in range(2)]
+        idx5 = load_list(offs5, "idx5")
+        weather(0, 0)
+        weather(0, 1)
+        wa_q[0, 1] = quantise_weight(raws[0], "wa01", "q10")
+        weather(0, 2)
+        wa_q[1, 1] = quantise_weight(raws[1], "wa11", "q11")
+        weather(0, 3)
+
+        ws_q = {}
+        for t in range(PACK):
+            g, a = t % 2, t // 2
+            raw = load_rows(ws, g, a, "ws%d%d" % (g, a))
+            weather(1, t)
+            ws_q[g, a] = quantise_weight(raw, "ws%d%d" % (g, a), "ws%d%d" % (g, a))
+
+        load_scale_rows(wr_plane, wr_scales)
+        wr_raw = stream.tile([P, 2, H], I32, name="wr_raw", tag="big", align_bytes=64)
+        nc.sync.dma_start(out=wr_raw[:], in_=wr_words.rearrange("g p c i -> p g (c i)").bitcast(I32))
+        wr_c = keep.tile([P, 2 * H], I32, name="wr_c", align_bytes=64)
+        wr_s = keep.tile([P, H], U8, name="wr_s", align_bytes=64)
+        nc.vector.tensor_copy(
+            out=wr_c[:].rearrange("p (b t m i) -> p b m t i", t=PACK, m=32, i=4),
+            in_=wr_raw[:].rearrange("p g c -> p (g c)").rearrange("p (b m i t) -> p b m t i", t=PACK, m=32, i=4),
+        )
+        nc.vector.tensor_copy(
+            out=wr_s[:].rearrange("p (b t m) -> p b m t", t=PACK, m=P),
+            in_=wr_plane[:].rearrange("p (b m t) -> p b m t", t=PACK, m=P),
+        )
+
+        xs, z_q = {}, {}
+
+        def read_slots(a, c):
+            e = load_rows(ex, a, c, "ex%d%d" % (a, c))
+            x = keep.tile([P, PACK, NB], F32, name="x%d%d" % (a, c), align_bytes=64)
+            zf = flat.tile([P, PACK, NB], BF16, name="zf", tag="zf")
+            for t in range(PACK):
+                nc.vector.tensor_copy(x[:, t, :], pages[a, t][:].indirect(idx5[:, 32 * c : 32 * (c + 1)]))
+            nc.vector.tensor_tensor(zf[:], x[:], e[:], MULT)
+            z = woven.tile([P, PACK * NB], BF16, name="z", tag="woven", align_bytes=64)
+            nc.scalar.copy(
+                out=z[:].rearrange("p (c i t) -> p c t i", i=4, t=PACK),
+                in_=zf[:].rearrange("p t (c i) -> p c t i", i=4),
+            )
+            xs[a, c] = x
+            z_q[a, c] = quantise(z, "z%d%d" % (a, c), "q%d%d" % (a, c))
+
+        def scores(a, c):
+            o = keep.tile([P, PACK, NB], F32, name="o%d%d" % (a, c), tag="page0%d" % (2 * c + a), align_bytes=64)
+            for t in range(PACK):
+                y = psum.tile([P, NB], F32, name="acc", tag="acc")
+                rest = psum.tile([P, NB], F32, name="acc", tag="acc")
+                for g in range(2):
+                    codes, scales = ws_q[g, a]
+                    nc.tensor.matmul_mx(
+                        out=y[:],
+                        lhsT=codes[:, P * t : P * (t + 1)].bitcast(FP8X4),
+                        lhsT_scale=scales[:, P * t : P * (t + 1)],
+                        rhs=z_q[g, c][0][:].bitcast(FP8X4),
+                        rhs_scale=z_q[g, c][1][:],
+                        start=(g == 0),
+                        stop=(g == 1),
+                    )
+                for g in range(2):
+                    col = KP * a + P * t
+                    nc.tensor.matmul_mx(
+                        out=rest[:],
+                        lhsT=wr_c[:, H * g + col : H * g + col + P].bitcast(FP8X4),
+                        lhsT_scale=wr_s[4 * g :, col : col + P],
+                        rhs=z_q[g, c][0][:].bitcast(FP8X4),
+                        rhs_scale=z_q[g, c][1][:],
+                        start=(g == 0),
+                        stop=(g == 1),
+                    )
+                nc.vector.tensor_tensor(o[:, t, :], y[:], xs[a, c][:, t, :], MULT)
+                nc.vector.tensor_tensor(o[:, t, :], rest[:], o[:, t, :], ADD)
+                nc.sync.dma_start(
+                    out=out.rearrange("(a p t) m -> a t p m", a=2, t=PACK)[a, t][:, NB * c : NB * (c + 1)],
+                    in_=o[:, t, :],
+                )
+
+        read_slots(0, 0)
+        read_slots(0, 1)
+        read_slots(1, 0)
+        read_slots(1, 1)
+        for c in range(2):
+            for a in range(2):
+                scores(a, c)

@@ -21,6 +21,7 @@ P = 128
 PACK = 4
 KP = P * PACK
 NB = 512
+CH = 256
 
 
 def tile_list_deicing_slot_scores_kernel(
@@ -32,9 +33,9 @@ def tile_list_deicing_slot_scores_kernel(
         lists = ctx.enter_context(tc.tile_pool(name="lists", bufs=1))
         keep = ctx.enter_context(tc.tile_pool(name="keep", bufs=1))
         stream = ctx.enter_context(tc.tile_pool(name="stream", bufs=5))
-        woven = ctx.enter_context(tc.tile_pool(name="woven", bufs=3))
-        flat = ctx.enter_context(tc.tile_pool(name="flat", bufs=2))
-        feat = ctx.enter_context(tc.tile_pool(name="feat", bufs=4))
+        woven = ctx.enter_context(tc.tile_pool(name="woven", bufs=4))
+        flat = ctx.enter_context(tc.tile_pool(name="flat", bufs=3))
+        feat = ctx.enter_context(tc.tile_pool(name="feat", bufs=8))
         psum = ctx.enter_context(tc.psum_pool(name="psum", bufs=8))
 
         def load_list(src, name):
@@ -42,15 +43,15 @@ def tile_list_deicing_slot_scores_kernel(
             nc.sync.dma_start(t[:], src)
             return t
 
-        def zeroed_plane(width, name):
+        def zeroed_plane(engine, width, name):
             t = keep.tile([P, width], U8, name=name, align_bytes=64)
-            nc.vector.memset(t[:].bitcast(I32), 0)
+            engine.memset(t[:].bitcast(I32), 0)
             return t
 
-        def load_scale_rows(plane, src):
+        def load_scale_rows(queue, plane, src):
             passes = src.shape[0]
             for q in range(4):
-                nc.sync.dma_start(
+                queue.dma_start(
                     out=plane[32 * q : 32 * q + 4 * passes, :].bitcast(I32),
                     in_=src[:, 4 * q : 4 * q + 4, :].bitcast(I32),
                 )
@@ -92,52 +93,55 @@ def tile_list_deicing_slot_scores_kernel(
             nc.sync.dma_start(out=pg[:], in_=page0.rearrange("(a p t) c -> a t p c", a=2, t=PACK)[a, t])
             return pg
 
-        def load_gain(src, name):
-            t = keep.tile([P, PACK, S], F32, name=name)
+        def load_gain(src, t0, t1, name):
+            t = keep.tile([P, t1 - t0, S], F32, name=name, align_bytes=64)
             for q in range(4):
                 nc.sync.dma_start(
-                    out=t[32 * q : 32 * (q + 1), :, :], in_=src.rearrange("(q t) j -> q t j", t=PACK)
+                    out=t[32 * q : 32 * (q + 1), :, :], in_=src.rearrange("(q t) j -> q t j", t=PACK)[:, t0:t1, :]
                 )
             return t
 
-        tab2_plane = zeroed_plane(T, "tab2_plane")
-        wf_plane = zeroed_plane(H, "wf_plane")
-        tab_plane = zeroed_plane(T, "tab_plane")
-        wr_plane = zeroed_plane(H, "wr_plane")
+        wf_plane = zeroed_plane(nc.gpsimd, H, "wf_plane")
+        tab2_plane = zeroed_plane(nc.gpsimd, T, "tab2_plane")
+        tab_plane = zeroed_plane(nc.vector, T, "tab_plane")
+        wr_plane = zeroed_plane(nc.vector, H, "wr_plane")
 
-        idx2 = load_list(offs2, "idx2")
-        wf_raw = keep.tile([P, 2 * H], U8, name="wf_raw", align_bytes=64)
-        nc.sync.dma_start(out=wf_raw[:].bitcast(I32), in_=wf_words[0].bitcast(I32))
-        tab2_w = load_table_words(tab2_words[0], "tab2_w")
-        load_scale_rows(wf_plane, wf_scales)
-        load_scale_rows(tab2_plane, tab2_scales)
-        idx4 = load_list(offs4, "idx4")
-        gain = lists.tile([P, 2, PACK], F32, name="gain")
-        nc.sync.dma_start(out=gain[:], in_=gf.rearrange("(a p t) -> p a t", a=2, t=PACK))
-        pages = {}
-        pages[0, 0] = load_page(0, 0)
-        g2 = load_gain(wg2, "g2")
+        def load_wf(a):
+            raw = keep.tile([P, 2 * KP], U8, name="wf_raw%d" % a, align_bytes=64)
+            nc.sync.dma_start(out=raw[:].bitcast(I32), in_=wf_words[0][:, 2 * KP * a : 2 * KP * (a + 1)].bitcast(I32))
+            return raw
 
         wf_c, wf_s = [], []
 
-        def deal_wf(a):
+        def deal_wf(a, raw):
             c = keep.tile([P, 2 * KP], U8, name="wf_c%d" % a, align_bytes=64)
             s = keep.tile([P, KP], U8, name="wf_s%d" % a, align_bytes=64)
             nc.vector.tensor_copy(
-                out=c[:].rearrange("p (t m e) -> p m t e", t=PACK, e=2),
-                in_=wf_raw[:, 2 * KP * a : 2 * KP * (a + 1)].rearrange("p (m t e) -> p m t e", t=PACK, e=2),
+                out=c[:].rearrange("p (t m e) -> p t m e", t=PACK, e=2),
+                in_=raw[:].rearrange("p (m t e) -> p t m e", t=PACK, e=2),
             )
             nc.vector.tensor_copy(
-                out=s[:].rearrange("p (t m) -> p m t", t=PACK),
-                in_=wf_plane[:, KP * a : KP * (a + 1)].rearrange("p (m t) -> p m t", t=PACK),
+                out=s[:].rearrange("p (t m) -> p t m", t=PACK),
+                in_=wf_plane[:, KP * a : KP * (a + 1)].rearrange("p (m t) -> p t m", t=PACK),
             )
             wf_c.append(c)
             wf_s.append(s)
 
-        deal_wf(0)
+        pages = {}
+        wf_raw0 = load_wf(0)
+        idx2 = load_list(offs2, "idx2")
+        load_scale_rows(nc.sync, wf_plane, wf_scales)
+        load_scale_rows(nc.gpsimd, tab2_plane, tab2_scales)
+        tab2_w = load_table_words(tab2_words[0], "tab2_w")
+        pages[0, 0] = load_page(0, 0)
+        g2 = load_gain(wg2, 0, PACK, "g2")
+        idx4 = load_list(offs4, "idx4")
+        gain = lists.tile([P, 2, PACK], F32, name="gain")
+        nc.sync.dma_start(out=gain[:], in_=gf.rearrange("(a p t) -> p a t", a=2, t=PACK))
+
+        deal_wf(0, wf_raw0)
         v2_c = gather(tab2_w, idx2, U32, "v2_c")
         v2_s = gather(tab2_plane, idx2, U8, "v2_s")
-        deal_wf(1)
 
         def frost(a, t):
             acc = psum.tile([P, NB], F32, name="acc", tag="acc")
@@ -152,40 +156,47 @@ def tile_list_deicing_slot_scores_kernel(
             )
             h = feat.tile([P, S], F32, name="h", tag="h")
             nc.scalar.activation(out=h[:], in_=acc[:], func=ACT.Gelu_apprx_tanh)
-            nc.scalar.activation(out=h[:], in_=h[:], func=ACT.Copy, scale=gain[:, a, t : t + 1])
-            nc.vector.tensor_tensor(pages[a, t][:].indirect(idx4[:]), h[:], g2[:, t, :], MULT)
+            if (a, t) == (0, 0):
+                factor = feat.tile([P, S], F32, name="factor", tag="h")
+                nc.vector.tensor_scalar_mul(factor[:], g2[:, t, :], gain[:, a, t : t + 1])
+                factor = factor[:]
+            else:
+                nc.scalar.activation(out=h[:], in_=h[:], func=ACT.Copy, scale=gain[:, a, t : t + 1])
+                factor = g2[:, t, :]
+            nc.vector.tensor_tensor(pages[a, t][:].indirect(idx4[:]), h[:], factor, MULT)
 
         v_c, wa_q = [], {}
         frost(0, 0)
         pages[0, 1] = load_page(0, 1)
         frost(0, 1)
         pages[0, 2] = load_page(0, 2)
+        deal_wf(1, load_wf(1))
         idx = load_list(offs, "idx")
         tab_w0 = load_table_words(tab_words[0], "tab_w0")
         frost(0, 2)
         pages[0, 3] = load_page(0, 3)
-        tab_w1 = load_table_words(tab_words[1], "tab_w1")
-        load_scale_rows(tab_plane, tab_scales)
+        raw00 = load_rows(wa, 0, 0, "wa00")
         frost(0, 3)
         v_c.append(gather(tab_w0, idx, U32, "v_c0"))
         pages[1, 0] = load_page(1, 0)
-        raw00 = load_rows(wa, 0, 0, "wa00")
+        tab_w1 = load_table_words(tab_words[1], "tab_w1")
+        load_scale_rows(nc.sync, tab_plane, tab_scales)
         frost(1, 0)
-        v_c.append(gather(tab_w1, idx, U32, "v_c1"))
+        wa_q[0, 0] = quantise_weight(raw00, "wa00", "q00")
         pages[1, 1] = load_page(1, 1)
         raw10 = load_rows(wa, 1, 0, "wa10")
         frost(1, 1)
+        v_c.append(gather(tab_w1, idx, U32, "v_c1"))
         v_s = gather(tab_plane, idx, U8, "v_s")
-        wa_q[0, 0] = quantise_weight(raw00, "wa00", "q00")
-        pages[1, 2] = load_page(1, 2)
         idx3 = load_list(offs3, "idx3")
-        g1 = load_gain(wg1, "g1")
-        frost(1, 2)
+        g1lo = load_gain(wg1, 0, 2, "g1lo")
+        pages[1, 2] = load_page(1, 2)
         wa_q[1, 0] = quantise_weight(raw10, "wa10", "q01")
+        frost(1, 2)
         pages[1, 3] = load_page(1, 3)
         frost(1, 3)
 
-        def weather(a, t):
+        def weather(a, t, last=False):
             acc = psum.tile([P, NB], F32, name="acc", tag="acc")
             for g in range(2):
                 codes, scales = wa_q[g, a]
@@ -198,27 +209,31 @@ def tile_list_deicing_slot_scores_kernel(
                     start=(g == 0),
                     stop=(g == 1),
                 )
-            h = feat.tile([P, S], F32, name="h", tag="h")
+            if last:
+                h = keep.tile([P, S], F32, name="h_last", tag="wr_plane", align_bytes=64)
+            else:
+                h = feat.tile([P, S], F32, name="h", tag="h")
             nc.scalar.activation(out=h[:], in_=acc[:], func=ACT.Abs)
-            nc.vector.tensor_tensor(pages[a, t][:].indirect(idx3[:]), h[:], g1[:, t, :], MULT)
+            nc.vector.tensor_tensor(pages[a, t][:].indirect(idx3[:]), h[:], g1[t // 2][:, t % 2, :], MULT)
 
         raws = [load_rows(wa, g, 1, "wa%d1" % g) for g in range(2)]
         idx5 = load_list(offs5, "idx5")
+        g1 = [g1lo]
         weather(0, 0)
         weather(0, 1)
         wa_q[0, 1] = quantise_weight(raws[0], "wa01", "q10")
-        weather(0, 2)
         wa_q[1, 1] = quantise_weight(raws[1], "wa11", "q11")
+        ws_raw = load_rows(ws, 0, 0, "ws00")
+        g1.append(load_gain(wg1, 2, PACK, "g1hi"))
+        weather(0, 2)
         weather(0, 3)
-
-        ws_q = {}
-        for t in range(PACK):
-            g, a = t % 2, t // 2
+        ws_q = {(0, 0): quantise_weight(ws_raw, "ws00", "ws00")}
+        for t, (g, a) in enumerate(((1, 0), (0, 1), (1, 1))):
             raw = load_rows(ws, g, a, "ws%d%d" % (g, a))
             weather(1, t)
             ws_q[g, a] = quantise_weight(raw, "ws%d%d" % (g, a), "ws%d%d" % (g, a))
 
-        load_scale_rows(wr_plane, wr_scales)
+        load_scale_rows(nc.sync, wr_plane, wr_scales)
         wr_raw = stream.tile([P, 2, H], I32, name="wr_raw", tag="big", align_bytes=64)
         nc.sync.dma_start(out=wr_raw[:], in_=wr_words.rearrange("g p c i -> p g (c i)").bitcast(I32))
         wr_c = keep.tile([P, 2 * H], I32, name="wr_c", align_bytes=64)
@@ -228,65 +243,105 @@ def tile_list_deicing_slot_scores_kernel(
             in_=wr_raw[:].rearrange("p g c -> p (g c)").rearrange("p (b m i t) -> p b m t i", t=PACK, m=32, i=4),
         )
         nc.vector.tensor_copy(
-            out=wr_s[:].rearrange("p (b t m) -> p b m t", t=PACK, m=P),
-            in_=wr_plane[:].rearrange("p (b m t) -> p b m t", t=PACK, m=P),
+            out=wr_s[:].rearrange("p (b t m) -> p b t m", t=PACK, m=P),
+            in_=wr_plane[:].rearrange("p (b m t) -> p b t m", t=PACK, m=P),
         )
 
-        xs, z_q = {}, {}
+        weather(1, 3, last=True)
 
-        def read_slots(a, c):
-            e = load_rows(ex, a, c, "ex%d%d" % (a, c))
-            x = keep.tile([P, PACK, NB], F32, name="x%d%d" % (a, c), align_bytes=64)
-            zf = flat.tile([P, PACK, NB], BF16, name="zf", tag="zf")
-            for t in range(PACK):
-                nc.vector.tensor_copy(x[:, t, :], pages[a, t][:].indirect(idx5[:, 32 * c : 32 * (c + 1)]))
-            nc.vector.tensor_tensor(zf[:], x[:], e[:], MULT)
-            z = woven.tile([P, PACK * NB], BF16, name="z", tag="woven", align_bytes=64)
-            nc.scalar.copy(
-                out=z[:].rearrange("p (c i t) -> p c t i", i=4, t=PACK),
-                in_=zf[:].rearrange("p t (c i) -> p c t i", i=4),
-            )
-            xs[a, c] = x
-            z_q[a, c] = quantise(z, "z%d%d" % (a, c), "q%d%d" % (a, c))
-
-        def scores(a, c):
-            o = keep.tile([P, PACK, NB], F32, name="o%d%d" % (a, c), tag="page0%d" % (2 * c + a), align_bytes=64)
-            for t in range(PACK):
-                y = psum.tile([P, NB], F32, name="acc", tag="acc")
-                rest = psum.tile([P, NB], F32, name="acc", tag="acc")
-                for g in range(2):
-                    codes, scales = ws_q[g, a]
-                    nc.tensor.matmul_mx(
-                        out=y[:],
-                        lhsT=codes[:, P * t : P * (t + 1)].bitcast(FP8X4),
-                        lhsT_scale=scales[:, P * t : P * (t + 1)],
-                        rhs=z_q[g, c][0][:].bitcast(FP8X4),
-                        rhs_scale=z_q[g, c][1][:],
-                        start=(g == 0),
-                        stop=(g == 1),
-                    )
-                for g in range(2):
-                    col = KP * a + P * t
-                    nc.tensor.matmul_mx(
-                        out=rest[:],
-                        lhsT=wr_c[:, H * g + col : H * g + col + P].bitcast(FP8X4),
-                        lhsT_scale=wr_s[4 * g :, col : col + P],
-                        rhs=z_q[g, c][0][:].bitcast(FP8X4),
-                        rhs_scale=z_q[g, c][1][:],
-                        start=(g == 0),
-                        stop=(g == 1),
-                    )
-                nc.vector.tensor_tensor(o[:, t, :], y[:], xs[a, c][:, t, :], MULT)
-                nc.vector.tensor_tensor(o[:, t, :], rest[:], o[:, t, :], ADD)
-                nc.sync.dma_start(
-                    out=out.rearrange("(a p t) m -> a t p m", a=2, t=PACK)[a, t][:, NB * c : NB * (c + 1)],
-                    in_=o[:, t, :],
-                )
-
-        read_slots(0, 0)
-        read_slots(0, 1)
-        read_slots(1, 0)
-        read_slots(1, 1)
-        for c in range(2):
+        exs = {}
+        for half in range(2):
             for a in range(2):
-                scores(a, c)
+                exs[a, half] = load_rows(ex, a, half, "ex%d%d" % (a, half))
+        xs, zs, z_q = {}, {}, {}
+
+        x_tag = ("g1hi", "wr_plane", "g1lo", "g2")
+        z_tag = ("g1lo", "g2", "g1hi", "z_last")
+
+        def read_slots(c):
+            both = keep.tile([P, 2, PACK, CH], F32, name="x%d" % c, tag=x_tag[c], align_bytes=64)
+            zs[c] = keep.tile([P, 2, PACK * CH], BF16, name="z%d" % c, tag=z_tag[c], align_bytes=64)
+            cols = slice(CH * (c % 2), CH * (c % 2 + 1))
+            for a in range(2):
+                x = both[:, a]
+                zf = flat.tile([P, PACK, CH], BF16, name="zf", tag="zf")
+                for t in range(PACK):
+                    nc.vector.tensor_copy(x[:, t, :], pages[a, t][:].indirect(idx5[:, 16 * c : 16 * (c + 1)]))
+                    if t % 2 == 1:
+                        nc.gpsimd.tensor_tensor(
+                            zf[:, t - 1 : t + 1, :], x[:, t - 1 : t + 1, :], exs[a, c // 2][:, t - 1 : t + 1, cols], MULT
+                        )
+                nc.scalar.copy(
+                    out=zs[c][:, a, :].rearrange("p (c i t) -> p c t i", i=4, t=PACK),
+                    in_=zf[:].rearrange("p t (c i) -> p c t i", i=4),
+                )
+                xs[c, a] = x
+
+        def quantise_z(c):
+            codes = keep.tile([P, NB], U32, name="zc%d" % c, tag="q%d%dc" % (c // 2, c % 2), align_bytes=64)
+            scales = keep.tile([P, NB], U8, name="zs%d" % c, tag="q%d%ds" % (c // 2, c % 2), align_bytes=64)
+            nc.vector.quantize_mx(out=codes[:].bitcast(FP8X4), scales=scales[:], in_=zs[c][:].rearrange("p a w -> p (a w)"))
+            z_q[c] = codes, scales
+
+        def scores(c):
+            zc, zsc = z_q[c]
+            late = []
+            for u in range(4):
+                a, t0 = u // 2, 2 * (u % 2)
+                y = psum.tile([P, 2, CH], F32, name="acc", tag="acc")
+                rest = psum.tile([P, 2, CH], F32, name="acc", tag="acc")
+                for i in range(2):
+                    for g in range(2):
+                        codes, scales = ws_q[g, a]
+                        col = P * (t0 + i)
+                        nc.tensor.matmul_mx(
+                            out=y[:, i, :],
+                            lhsT=codes[:, col : col + P].bitcast(FP8X4),
+                            lhsT_scale=scales[:, col : col + P],
+                            rhs=zc[:, CH * g : CH * (g + 1)].bitcast(FP8X4),
+                            rhs_scale=zsc[:, CH * g : CH * (g + 1)],
+                            start=(g == 0),
+                            stop=(g == 1),
+                        )
+                for i in range(2):
+                    for g in range(2):
+                        col = KP * a + P * (t0 + i)
+                        nc.tensor.matmul_mx(
+                            out=rest[:, i, :],
+                            lhsT=wr_c[:, H * g + col : H * g + col + P].bitcast(FP8X4),
+                            lhsT_scale=wr_s[4 * g :, col : col + P],
+                            rhs=zc[:, CH * g : CH * (g + 1)].bitcast(FP8X4),
+                            rhs_scale=zsc[:, CH * g : CH * (g + 1)],
+                            start=(g == 0),
+                            stop=(g == 1),
+                        )
+                o = feat.tile([P, 2, CH], F32, name="o", tag="h")
+                dst = out.rearrange("(a p t) m -> a p t m", a=2, t=PACK)[a][:, t0 : t0 + 2, CH * c : CH * (c + 1)]
+                nc.vector.tensor_tensor(o[:], y[:], xs[c, a][:, t0 : t0 + 2, :], MULT)
+                for o2, rest2, dst2 in late:
+                    nc.vector.tensor_tensor(o2[:], rest2[:], o2[:], ADD)
+                    nc.sync.dma_start(out=dst2, in_=o2[:])
+                late = []
+                if u < (0,0,0,0)[c]:
+                    r = flat.tile([P, 2, CH], F32, name="r", tag="r")
+                    nc.scalar.copy(out=r[:], in_=rest[:])
+                    nc.gpsimd.tensor_tensor(o[:], r[:], o[:], ADD)
+                    nc.sync.dma_start(out=dst, in_=o[:])
+                else:
+                    late.append((o, rest, dst))
+            for o2, rest2, dst2 in late:
+                nc.vector.tensor_tensor(o2[:], rest2[:], o2[:], ADD)
+                nc.sync.dma_start(out=dst2, in_=o2[:])
+
+        read_slots(0)
+        read_slots(1)
+        quantise_z(0)
+        read_slots(2)
+        quantise_z(1)
+        scores(0)
+        read_slots(3)
+        quantise_z(2)
+        scores(1)
+        quantise_z(3)
+        scores(2)
+        scores(3)

@@ -101,54 +101,48 @@ def tile_list_deicing_slot_scores_kernel(
                 )
             return t
 
-        wf_plane = zeroed_plane(nc.gpsimd, H, "wf_plane")
-        tab2_plane = zeroed_plane(nc.gpsimd, T, "tab2_plane")
+        wf_plane = zeroed_plane(nc.vector, H, "wf_plane")
+        tab2_plane = zeroed_plane(nc.vector, T, "tab2_plane")
         tab_plane = zeroed_plane(nc.vector, T, "tab_plane")
         wr_plane = zeroed_plane(nc.vector, H, "wr_plane")
 
-        def load_wf(a):
-            raw = keep.tile([P, 2 * KP], U8, name="wf_raw%d" % a, align_bytes=64)
-            nc.sync.dma_start(out=raw[:].bitcast(I32), in_=wf_words[0][:, 2 * KP * a : 2 * KP * (a + 1)].bitcast(I32))
-            return raw
-
-        wf_c, wf_s = [], []
-
-        def deal_wf(a, raw):
-            c = keep.tile([P, 2 * KP], U8, name="wf_c%d" % a, align_bytes=64)
-            s = keep.tile([P, KP], U8, name="wf_s%d" % a, align_bytes=64)
+        def deal_wf_words(a, tag):
+            c = keep.tile([P, 2 * KP], U8, name="wf_c%d" % a, tag=tag, align_bytes=64)
             nc.vector.tensor_copy(
                 out=c[:].rearrange("p (t m e) -> p t m e", t=PACK, e=2),
-                in_=raw[:].rearrange("p (m t e) -> p t m e", t=PACK, e=2),
+                in_=wf_raw[:, 2 * KP * a : 2 * KP * (a + 1)].rearrange("p (m t e) -> p t m e", t=PACK, e=2),
             )
-            nc.vector.tensor_copy(
-                out=s[:].rearrange("p (t m) -> p t m", t=PACK),
-                in_=wf_plane[:, KP * a : KP * (a + 1)].rearrange("p (m t) -> p t m", t=PACK),
-            )
-            wf_c.append(c)
-            wf_s.append(s)
+            return c
 
         pages = {}
-        wf_raw0 = load_wf(0)
+        wf_raw = keep.tile([P, 2 * H], U8, name="wf_raw", align_bytes=64)
+        nc.sync.dma_start(out=wf_raw[:].bitcast(I32), in_=wf_words[0].bitcast(I32))
         idx2 = load_list(offs2, "idx2")
         load_scale_rows(nc.sync, wf_plane, wf_scales)
-        load_scale_rows(nc.gpsimd, tab2_plane, tab2_scales)
         tab2_w = load_table_words(tab2_words[0], "tab2_w")
+        load_scale_rows(nc.sync, tab2_plane, tab2_scales)
         pages[0, 0] = load_page(0, 0)
-        g2 = load_gain(wg2, 0, PACK, "g2")
         idx4 = load_list(offs4, "idx4")
         gain = lists.tile([P, 2, PACK], F32, name="gain")
         nc.sync.dma_start(out=gain[:], in_=gf.rearrange("(a p t) -> p a t", a=2, t=PACK))
+        g2 = [load_gain(wg2, 0, 1, "g2first")[:, 0, :]]
 
-        deal_wf(0, wf_raw0)
+        wf_s = keep.tile([P, H], U8, name="wf_s", align_bytes=64)
+        nc.vector.tensor_copy(
+            out=wf_s[:].rearrange("p (b t m) -> p b t m", t=PACK, m=P),
+            in_=wf_plane[:].rearrange("p (b m t) -> p b t m", t=PACK, m=P),
+        )
+        wf_c = [deal_wf_words(0, "wf_c0")]
         v2_c = gather(tab2_w, idx2, U32, "v2_c")
         v2_s = gather(tab2_plane, idx2, U8, "v2_s")
+        wf_c.append(deal_wf_words(1, "tab2_plane"))
 
         def frost(a, t):
             acc = psum.tile([P, NB], F32, name="acc", tag="acc")
             nc.tensor.matmul_mx(
                 out=acc[:],
                 lhsT=wf_c[a][:, 2 * P * t : 2 * P * (t + 1)].bitcast(FP4X4),
-                lhsT_scale=wf_s[a][:, P * t : P * (t + 1)],
+                lhsT_scale=wf_s[:, KP * a + P * t : KP * a + P * (t + 1)],
                 rhs=v2_c[:].bitcast(FP8X4),
                 rhs_scale=v2_s[:],
                 start=True,
@@ -158,41 +152,36 @@ def tile_list_deicing_slot_scores_kernel(
             nc.scalar.activation(out=h[:], in_=acc[:], func=ACT.Gelu_apprx_tanh)
             if (a, t) == (0, 0):
                 factor = feat.tile([P, S], F32, name="factor", tag="h")
-                nc.vector.tensor_scalar_mul(factor[:], g2[:, t, :], gain[:, a, t : t + 1])
+                nc.vector.tensor_scalar_mul(factor[:], g2[t], gain[:, a, t : t + 1])
                 factor = factor[:]
             else:
                 nc.scalar.activation(out=h[:], in_=h[:], func=ACT.Copy, scale=gain[:, a, t : t + 1])
-                factor = g2[:, t, :]
+                factor = g2[t]
             nc.vector.tensor_tensor(pages[a, t][:].indirect(idx4[:]), h[:], factor, MULT)
 
         v_c, wa_q = [], {}
         frost(0, 0)
+        rest2 = load_gain(wg2, 1, PACK, "g2")
+        g2.extend(rest2[:, t, :] for t in range(PACK - 1))
         pages[0, 1] = load_page(0, 1)
         frost(0, 1)
         pages[0, 2] = load_page(0, 2)
-        deal_wf(1, load_wf(1))
-        idx = load_list(offs, "idx")
-        tab_w0 = load_table_words(tab_words[0], "tab_w0")
         frost(0, 2)
+        idx = load_list(offs, "idx")
+        v_c.append(gather(load_table_words(tab_words[0], "tab_w0"), idx, U32, "v_c0"))
         pages[0, 3] = load_page(0, 3)
-        raw00 = load_rows(wa, 0, 0, "wa00")
         frost(0, 3)
-        v_c.append(gather(tab_w0, idx, U32, "v_c0"))
+        wa_q[0, 0] = quantise_weight(load_rows(wa, 0, 0, "wa00"), "wa00", "q00")
         pages[1, 0] = load_page(1, 0)
-        tab_w1 = load_table_words(tab_words[1], "tab_w1")
-        load_scale_rows(nc.sync, tab_plane, tab_scales)
         frost(1, 0)
-        wa_q[0, 0] = quantise_weight(raw00, "wa00", "q00")
+        wa_q[1, 0] = quantise_weight(load_rows(wa, 1, 0, "wa10"), "wa10", "q01")
         pages[1, 1] = load_page(1, 1)
-        raw10 = load_rows(wa, 1, 0, "wa10")
         frost(1, 1)
-        v_c.append(gather(tab_w1, idx, U32, "v_c1"))
-        v_s = gather(tab_plane, idx, U8, "v_s")
-        idx3 = load_list(offs3, "idx3")
-        g1lo = load_gain(wg1, 0, 2, "g1lo")
+        v_c.append(gather(load_table_words(tab_words[1], "tab_w1"), idx, U32, "v_c1"))
         pages[1, 2] = load_page(1, 2)
-        wa_q[1, 0] = quantise_weight(raw10, "wa10", "q01")
         frost(1, 2)
+        load_scale_rows(nc.sync, tab_plane, tab_scales)
+        v_s = gather(tab_plane, idx, U8, "v_s")
         pages[1, 3] = load_page(1, 3)
         frost(1, 3)
 
@@ -210,28 +199,27 @@ def tile_list_deicing_slot_scores_kernel(
                     stop=(g == 1),
                 )
             if last:
-                h = keep.tile([P, S], F32, name="h_last", tag="wr_plane", align_bytes=64)
+                h = keep.tile([P, S], F32, name="h_last", align_bytes=64)
             else:
                 h = feat.tile([P, S], F32, name="h", tag="h")
             nc.scalar.activation(out=h[:], in_=acc[:], func=ACT.Abs)
-            nc.vector.tensor_tensor(pages[a, t][:].indirect(idx3[:]), h[:], g1[t // 2][:, t % 2, :], MULT)
+            nc.vector.tensor_tensor(pages[a, t][:].indirect(idx3[:]), h[:], g1[t], MULT)
 
-        raws = [load_rows(wa, g, 1, "wa%d1" % g) for g in range(2)]
-        idx5 = load_list(offs5, "idx5")
-        g1 = [g1lo]
+        idx3 = load_list(offs3, "idx3")
+        first = load_gain(wg1, 0, 2, "g1lo")
+        g1 = [first[:, 0, :], first[:, 1, :]]
         weather(0, 0)
         weather(0, 1)
-        wa_q[0, 1] = quantise_weight(raws[0], "wa01", "q10")
-        wa_q[1, 1] = quantise_weight(raws[1], "wa11", "q11")
-        ws_raw = load_rows(ws, 0, 0, "ws00")
-        g1.append(load_gain(wg1, 2, PACK, "g1hi"))
+        wa_q[0, 1] = quantise_weight(load_rows(wa, 0, 1, "wa01"), "wa01", "q10")
+        wa_q[1, 1] = quantise_weight(load_rows(wa, 1, 1, "wa11"), "wa11", "q11")
+        g1.append(load_gain(wg1, 2, 3, "g1mid")[:, 0, :])
         weather(0, 2)
-        weather(0, 3)
-        ws_q = {(0, 0): quantise_weight(ws_raw, "ws00", "ws00")}
-        for t, (g, a) in enumerate(((1, 0), (0, 1), (1, 1))):
-            raw = load_rows(ws, g, a, "ws%d%d" % (g, a))
+        for t in range(3):
             weather(1, t)
-            ws_q[g, a] = quantise_weight(raw, "ws%d%d" % (g, a), "ws%d%d" % (g, a))
+        ws_q = {}
+        for a in range(2):
+            for g in range(2):
+                ws_q[g, a] = quantise_weight(load_rows(ws, g, a, "ws%d%d" % (g, a)), "ws%d%d" % (g, a), "ws%d%d" % (g, a))
 
         load_scale_rows(nc.sync, wr_plane, wr_scales)
         wr_raw = stream.tile([P, 2, H], I32, name="wr_raw", tag="big", align_bytes=64)
@@ -247,15 +235,18 @@ def tile_list_deicing_slot_scores_kernel(
             in_=wr_plane[:].rearrange("p (b m t) -> p b t m", t=PACK, m=P),
         )
 
+        g1.append(load_gain(wg1, 3, PACK, "g1hi")[:, 0, :])
+        weather(0, 3)
         weather(1, 3, last=True)
 
+        idx5 = load_list(offs5, "idx5")
         exs = {}
         for half in range(2):
             for a in range(2):
                 exs[a, half] = load_rows(ex, a, half, "ex%d%d" % (a, half))
         xs, zs, z_q = {}, {}, {}
 
-        x_tag = ("g1hi", "wr_plane", "g1lo", "g2")
+        x_tag = ("g1hi", "h_last", "g1lo", "g2")
         z_tag = ("g1lo", "g2", "g1hi", "z_last")
 
         def read_slots(c):
@@ -322,7 +313,7 @@ def tile_list_deicing_slot_scores_kernel(
                     nc.vector.tensor_tensor(o2[:], rest2[:], o2[:], ADD)
                     nc.sync.dma_start(out=dst2, in_=o2[:])
                 late = []
-                if u < (0,0,0,0)[c]:
+                if u < (0,2,2,1)[c]:
                     r = flat.tile([P, 2, CH], F32, name="r", tag="r")
                     nc.scalar.copy(out=r[:], in_=rest[:])
                     nc.gpsimd.tensor_tensor(o[:], r[:], o[:], ADD)

@@ -1,6 +1,7 @@
 from contextlib import ExitStack
 
 import concourse.mybir as mybir
+from concourse.masks import make_identity
 
 K1, K2, H, T, S, T2, M = 1024, 512, 1024, 2048, 512, 2048, 1024
 FLOPS = 2 * (K1 * H * S + K2 * H * S + 2 * H * H * M)
@@ -36,7 +37,8 @@ def tile_list_deicing_slot_scores_kernel(
         woven = ctx.enter_context(tc.tile_pool(name="woven", bufs=4))
         flat = ctx.enter_context(tc.tile_pool(name="flat", bufs=3))
         feat = ctx.enter_context(tc.tile_pool(name="feat", bufs=8))
-        psum = ctx.enter_context(tc.psum_pool(name="psum", bufs=8))
+        psum = ctx.enter_context(tc.psum_pool(name="psum", bufs=7))
+        side = ctx.enter_context(tc.psum_pool(name="side", bufs=1))
 
         def load_list(src, name):
             t = lists.tile(list(src.shape), U16, name=name)
@@ -66,8 +68,8 @@ def tile_list_deicing_slot_scores_kernel(
             nc.vector.tensor_copy(t[:], window[:].indirect(offsets[:]))
             return t
 
-        def load_rows(src, g, c, name):
-            t = stream.tile([P, PACK, NB], F32, name=name, tag="big", align_bytes=64)
+        def load_rows(src, g, c, name, pool=stream, tag="big"):
+            t = pool.tile([P, PACK, NB], F32, name=name, tag=tag, align_bytes=64)
             nc.sync.dma_start(
                 out=t[:],
                 in_=src[KP * g : KP * (g + 1), NB * c : NB * (c + 1)].rearrange("(p j) c -> p j c", j=PACK),
@@ -93,13 +95,28 @@ def tile_list_deicing_slot_scores_kernel(
             nc.sync.dma_start(out=pg[:], in_=page0.rearrange("(a p t) c -> a t p c", a=2, t=PACK)[a, t])
             return pg
 
-        def load_gain(src, t0, t1, name):
-            t = keep.tile([P, t1 - t0, S], F32, name=name, align_bytes=64)
-            for q in range(4):
-                nc.sync.dma_start(
-                    out=t[32 * q : 32 * (q + 1), :, :], in_=src.rearrange("(q t) j -> q t j", t=PACK)[:, t0:t1, :]
-                )
-            return t
+        ident = keep.tile([P, P], F32, name="ident")
+        make_identity(nc, ident[:])
+
+        def load_factor(src, name):
+            rows = keep.tile([P, S], F32, name=name + "_rows", tag="factor_rows")
+            nc.sync.dma_start(out=rows[:], in_=src)
+            return rows
+
+        def turn_factor(rows):
+            turned = psum.tile([P, PACK, P], F32, name="acc", tag="acc")
+            for b in range(PACK):
+                nc.tensor.transpose(turned[:, b, :], rows[:, P * b : P * (b + 1)], ident[:])
+            return turned
+
+        def deal_factor(turned, t, bank_pool):
+            wide = keep.tile([P, PACK, 4, 32], F32, name="wide", tag="wide")
+            picked = turned[:].rearrange("p b (q t) -> p b t q", t=PACK)[:, :, t, :]
+            nc.scalar.copy(out=wide[:], in_=picked.unsqueeze(2).to_broadcast([P, PACK, 4, 32]))
+            back = bank_pool.tile([P, S], F32, name="acc", tag="acc")
+            for b in range(PACK):
+                nc.tensor.transpose(back[:, P * b : P * (b + 1)], wide[:, b].rearrange("p g q -> p (g q)"), ident[:])
+            return back
 
         wf_plane = zeroed_plane(nc.vector, H, "wf_plane")
         tab2_plane = zeroed_plane(nc.vector, T, "tab2_plane")
@@ -119,14 +136,23 @@ def tile_list_deicing_slot_scores_kernel(
         nc.sync.dma_start(out=wf_raw[:].bitcast(I32), in_=wf_words[0].bitcast(I32))
         idx2 = load_list(offs2, "idx2")
         load_scale_rows(nc.sync, wf_plane, wf_scales)
+        wg2_rows = load_factor(wg2, "wg2")
         tab2_w = load_table_words(tab2_words[0], "tab2_w")
         load_scale_rows(nc.sync, tab2_plane, tab2_scales)
-        pages[0, 0] = load_page(0, 0)
-        idx4 = load_list(offs4, "idx4")
         gain = lists.tile([P, 2, PACK], F32, name="gain")
         nc.sync.dma_start(out=gain[:], in_=gf.rearrange("(a p t) -> p a t", a=2, t=PACK))
-        g2 = [load_gain(wg2, 0, 1, "g2first")[:, 0, :]]
+        pages[0, 0] = load_page(0, 0)
+        idx4 = load_list(offs4, "idx4")
 
+        g2 = [keep.tile([P, PACK, S], F32, name="g2_%d" % a, tag=("g2", "x_second")[a], align_bytes=64) for a in range(2)]
+        wg2_turned = turn_factor(wg2_rows)
+
+        def deal_frost_factor(t, bank_pool):
+            back = deal_factor(wg2_turned, t, bank_pool)
+            for a in range(2):
+                nc.scalar.activation(out=g2[a][:, t, :], in_=back[:], func=ACT.Copy, scale=gain[:, a, t : t + 1])
+
+        deal_frost_factor(0, psum)
         wf_s = keep.tile([P, H], U8, name="wf_s", align_bytes=64)
         nc.vector.tensor_copy(
             out=wf_s[:].rearrange("p (b t m) -> p b t m", t=PACK, m=P),
@@ -137,8 +163,8 @@ def tile_list_deicing_slot_scores_kernel(
         v2_s = gather(tab2_plane, idx2, U8, "v2_s")
         wf_c.append(deal_wf_words(1, "tab2_plane"))
 
-        def frost(a, t):
-            acc = psum.tile([P, NB], F32, name="acc", tag="acc")
+        def frost_features(a, t):
+            acc = (side if (a, t) == (0, 0) else psum).tile([P, NB], F32, name="acc", tag="acc")
             nc.tensor.matmul_mx(
                 out=acc[:],
                 lhsT=wf_c[a][:, 2 * P * t : 2 * P * (t + 1)].bitcast(FP4X4),
@@ -148,21 +174,22 @@ def tile_list_deicing_slot_scores_kernel(
                 start=True,
                 stop=True,
             )
-            h = feat.tile([P, S], F32, name="h", tag="h")
+            h = feat.tile([P, S], F32, name="h", tag="h", align_bytes=64)
             nc.scalar.activation(out=h[:], in_=acc[:], func=ACT.Gelu_apprx_tanh)
-            if (a, t) == (0, 0):
-                factor = feat.tile([P, S], F32, name="factor", tag="h")
-                nc.vector.tensor_scalar_mul(factor[:], g2[t], gain[:, a, t : t + 1])
-                factor = factor[:]
-            else:
-                nc.scalar.activation(out=h[:], in_=h[:], func=ACT.Copy, scale=gain[:, a, t : t + 1])
-                factor = g2[t]
-            nc.vector.tensor_tensor(pages[a, t][:].indirect(idx4[:]), h[:], factor, MULT)
+            return h
+
+        h2 = {(0, 0): frost_features(0, 0)}
+        for t in range(1, PACK):
+            deal_frost_factor(t, side)
+            h2[0, t] = frost_features(0, t)
+        for t in range(PACK):
+            h2[1, t] = frost_features(1, t)
+
+        def frost(a, t):
+            nc.vector.tensor_tensor(pages[a, t][:].indirect(idx4[:]), h2[a, t][:], g2[a][:, t, :], MULT)
 
         v_c, wa_q = [], {}
         frost(0, 0)
-        rest2 = load_gain(wg2, 1, PACK, "g2")
-        g2.extend(rest2[:, t, :] for t in range(PACK - 1))
         pages[0, 1] = load_page(0, 1)
         frost(0, 1)
         pages[0, 2] = load_page(0, 2)
@@ -171,6 +198,10 @@ def tile_list_deicing_slot_scores_kernel(
         v_c.append(gather(load_table_words(tab_words[0], "tab_w0"), idx, U32, "v_c0"))
         pages[0, 3] = load_page(0, 3)
         frost(0, 3)
+        wg1_turned = turn_factor(load_factor(wg1, "wg1"))
+        g1 = keep.tile([P, PACK, S], F32, name="g1", align_bytes=64)
+        for t in range(PACK):
+            nc.scalar.copy(out=g1[:, t, :], in_=deal_factor(wg1_turned, t, side)[:])
         wa_q[0, 0] = quantise_weight(load_rows(wa, 0, 0, "wa00"), "wa00", "q00")
         pages[1, 0] = load_page(1, 0)
         frost(1, 0)
@@ -185,7 +216,7 @@ def tile_list_deicing_slot_scores_kernel(
         pages[1, 3] = load_page(1, 3)
         frost(1, 3)
 
-        def weather(a, t, last=False):
+        def weather(a, t, pool=feat, tag="h"):
             acc = psum.tile([P, NB], F32, name="acc", tag="acc")
             for g in range(2):
                 codes, scales = wa_q[g, a]
@@ -198,23 +229,17 @@ def tile_list_deicing_slot_scores_kernel(
                     start=(g == 0),
                     stop=(g == 1),
                 )
-            if last:
-                h = keep.tile([P, S], F32, name="h_last", align_bytes=64)
-            else:
-                h = feat.tile([P, S], F32, name="h", tag="h")
+            h = pool.tile([P, S], F32, name="h", tag=tag, align_bytes=64)
             nc.scalar.activation(out=h[:], in_=acc[:], func=ACT.Abs)
-            nc.vector.tensor_tensor(pages[a, t][:].indirect(idx3[:]), h[:], g1[t], MULT)
+            nc.vector.tensor_tensor(pages[a, t][:].indirect(idx3[:]), h[:], g1[:, t, :], MULT)
 
-        idx3 = load_list(offs3, "idx3")
-        first = load_gain(wg1, 0, 2, "g1lo")
-        g1 = [first[:, 0, :], first[:, 1, :]]
-        weather(0, 0)
-        weather(0, 1)
         wa_q[0, 1] = quantise_weight(load_rows(wa, 0, 1, "wa01"), "wa01", "q10")
-        wa_q[1, 1] = quantise_weight(load_rows(wa, 1, 1, "wa11"), "wa11", "q11")
-        g1.append(load_gain(wg1, 2, 3, "g1mid")[:, 0, :])
-        weather(0, 2)
-        for t in range(3):
+        idx3 = load_list(offs3, "idx3")
+        for t in range(PACK - 1):
+            weather(0, t)
+        wa_q[1, 1] = quantise_weight(load_rows(wa, 1, 1, "wa11", keep, "z_first"), "wa11", "q11")
+        weather(0, PACK - 1, keep, "z_first")
+        for t in range(PACK):
             weather(1, t)
         ws_q = {}
         for a in range(2):
@@ -235,10 +260,6 @@ def tile_list_deicing_slot_scores_kernel(
             in_=wr_plane[:].rearrange("p (b m t) -> p b t m", t=PACK, m=P),
         )
 
-        g1.append(load_gain(wg1, 3, PACK, "g1hi")[:, 0, :])
-        weather(0, 3)
-        weather(1, 3, last=True)
-
         idx5 = load_list(offs5, "idx5")
         exs = {}
         for half in range(2):
@@ -246,8 +267,8 @@ def tile_list_deicing_slot_scores_kernel(
                 exs[a, half] = load_rows(ex, a, half, "ex%d%d" % (a, half))
         xs, zs, z_q = {}, {}, {}
 
-        x_tag = ("g1hi", "h_last", "g1lo", "g2")
-        z_tag = ("g1lo", "g2", "g1hi", "z_last")
+        x_tag = ("g1", "x_second", "z_first", "g2")
+        z_tag = ("z_first", "g2", "g1", "x_second")
 
         def read_slots(c):
             both = keep.tile([P, 2, PACK, CH], F32, name="x%d" % c, tag=x_tag[c], align_bytes=64)
@@ -280,7 +301,7 @@ def tile_list_deicing_slot_scores_kernel(
             for u in range(4):
                 a, t0 = u // 2, 2 * (u % 2)
                 y = psum.tile([P, 2, CH], F32, name="acc", tag="acc")
-                rest = psum.tile([P, 2, CH], F32, name="acc", tag="acc")
+                rest = (side if u == 3 else psum).tile([P, 2, CH], F32, name="acc", tag="acc")
                 for i in range(2):
                     for g in range(2):
                         codes, scales = ws_q[g, a]
@@ -306,7 +327,7 @@ def tile_list_deicing_slot_scores_kernel(
                             start=(g == 0),
                             stop=(g == 1),
                         )
-                o = feat.tile([P, 2, CH], F32, name="o", tag="h")
+                o = feat.tile([P, 2, CH], F32, name="o", tag="h", align_bytes=64)
                 dst = out.rearrange("(a p t) m -> a p t m", a=2, t=PACK)[a][:, t0 : t0 + 2, CH * c : CH * (c + 1)]
                 nc.vector.tensor_tensor(o[:], y[:], xs[c, a][:, t0 : t0 + 2, :], MULT)
                 for o2, rest2, dst2 in late:
@@ -314,7 +335,7 @@ def tile_list_deicing_slot_scores_kernel(
                     nc.sync.dma_start(out=dst2, in_=o2[:])
                 late = []
                 if u < (0,2,2,1)[c]:
-                    r = flat.tile([P, 2, CH], F32, name="r", tag="r")
+                    r = flat.tile([P, 2, CH], F32, name="r", tag="r", bufs=2)
                     nc.scalar.copy(out=r[:], in_=rest[:])
                     nc.gpsimd.tensor_tensor(o[:], r[:], o[:], ADD)
                     nc.sync.dma_start(out=dst, in_=o[:])

from contextlib import ExitStack

import concourse.mybir as mybir
from concourse.masks import make_identity

K1, K2, H, T, S, T2, M = 1024, 512, 1024, 2048, 512, 2048, 1024
FLOPS = 2 * (K1 * H * S + K2 * H * S + 2 * H * H * M)

F32 = mybir.dt.float32
BF16 = mybir.dt.bfloat16
I32 = mybir.dt.int32
U32 = mybir.dt.uint32
U16 = mybir.dt.uint16
U8 = mybir.dt.uint8
FP8X4 = mybir.dt.float8_e4m3fn_x4
FP4X4 = mybir.dt.float4_e2m1fn_x4
MULT = mybir.AluOpType.mult
ADD = mybir.AluOpType.add
ACT = mybir.ActivationFunctionType

P = 128
PACK = 4
KP = P * PACK
NB = 512
CH = 256


def tile_list_deicing_slot_scores_kernel(
    tc, tab_words, tab_scales, tab2_words, tab2_scales, offs, offs2, offs3, offs4, offs5,
    wa, wf_words, wf_scales, gf, page0, wg1, wg2, ex, ws, wr_words, wr_scales, out,
):
    nc = tc.nc
    with ExitStack() as ctx:
        lists = ctx.enter_context(tc.tile_pool(name="lists", bufs=1))
        keep = ctx.enter_context(tc.tile_pool(name="keep", bufs=1))
        stream = ctx.enter_context(tc.tile_pool(name="stream", bufs=5))
        woven = ctx.enter_context(tc.tile_pool(name="woven", bufs=4))
        flat = ctx.enter_context(tc.tile_pool(name="flat", bufs=3))
        feat = ctx.enter_context(tc.tile_pool(name="feat", bufs=8))
        psum = ctx.enter_context(tc.psum_pool(name="psum", bufs=7))
        side = ctx.enter_context(tc.psum_pool(name="side", bufs=1))

        def load_list(src, name):
            t = lists.tile(list(src.shape), U16, name=name)
            nc.sync.dma_start(t[:], src)
            return t

        def zeroed_plane(engine, width, name):
            t = keep.tile([P, width], U8, name=name, align_bytes=64)
            engine.memset(t[:].bitcast(I32), 0)
            return t

        def load_scale_rows(queue, plane, src):
            passes = src.shape[0]
            for q in range(4):
                queue.dma_start(
                    out=plane[32 * q : 32 * q + 4 * passes, :].bitcast(I32),
                    in_=src[:, 4 * q : 4 * q + 4, :].bitcast(I32),
                )

        def load_table_words(src, name):
            t = stream.tile([P, T], U32, name=name, tag="big", align_bytes=64)
            nc.sync.dma_start(out=t[:].bitcast(I32), in_=src.rearrange("p t i -> p (t i)").bitcast(I32))
            return t

        def gather(window, offsets, dtype, name):
            t = keep.tile([P, S], dtype, name=name, align_bytes=64)
            nc.vector.tensor_copy(t[:], window[:].indirect(offsets[:]))
            return t

        def load_rows(src, g, c, name, pool=stream, tag="big"):
            t = pool.tile([P, PACK, NB], F32, name=name, tag=tag, align_bytes=64)
            nc.sync.dma_start(
                out=t[:],
                in_=src[KP * g : KP * (g + 1), NB * c : NB * (c + 1)].rearrange("(p j) c -> p j c", j=PACK),
            )
            return t

        def quantise(src, name, tag):
            codes = keep.tile([P, NB], U32, name=name + "c", tag=tag + "c", align_bytes=64)
            scales = keep.tile([P, NB], U8, name=name + "s", tag=tag + "s", align_bytes=64)
            nc.vector.quantize_mx(out=codes[:].bitcast(FP8X4), scales=scales[:], in_=src[:])
            return codes, scales

        def quantise_weight(raw, name, tag):
            w = woven.tile([P, PACK * NB], BF16, name="w", tag="woven", align_bytes=64)
            nc.scalar.copy(
                out=w[:].rearrange("p (t m j) -> p m t j", t=PACK, j=PACK),
                in_=raw[:].rearrange("p j (m t) -> p m t j", t=PACK),
            )
            return quantise(w, name, tag)

        def load_page(a, t):
            pg = keep.tile([P, T2], F32, name="page%d%d" % (a, t), align_bytes=64)
            nc.sync.dma_start(out=pg[:], in_=page0.rearrange("(a p t) c -> a t p c", a=2, t=PACK)[a, t])
            return pg

        ident = keep.tile([P, P], F32, name="ident")
        make_identity(nc, ident[:])

        def load_factor(src, name):
            rows = keep.tile([P, S], F32, name=name + "_rows", tag="factor_rows")
            nc.sync.dma_start(out=rows[:], in_=src)
            return rows

        def turn_factor(rows):
            turned = psum.tile([P, PACK, P], F32, name="acc", tag="acc")
            for b in range(PACK):
                nc.tensor.transpose(turned[:, b, :], rows[:, P * b : P * (b + 1)], ident[:])
            return turned

        def deal_factor(turned, t, bank_pool):
            wide = keep.tile([P, PACK, 4, 32], F32, name="wide", tag="wide")
            picked = turned[:].rearrange("p b (q t) -> p b t q", t=PACK)[:, :, t, :]
            nc.scalar.copy(out=wide[:], in_=picked.unsqueeze(2).to_broadcast([P, PACK, 4, 32]))
            back = bank_pool.tile([P, S], F32, name="acc", tag="acc")
            for b in range(PACK):
                nc.tensor.transpose(back[:, P * b : P * (b + 1)], wide[:, b].rearrange("p g q -> p (g q)"), ident[:])
            return back

        wf_plane = zeroed_plane(nc.vector, H, "wf_plane")
        tab2_plane = zeroed_plane(nc.vector, T, "tab2_plane")
        tab_plane = zeroed_plane(nc.vector, T, "tab_plane")
        wr_plane = zeroed_plane(nc.vector, H, "wr_plane")

        def deal_wf_words(a, tag):
            c = keep.tile([P, 2 * KP], U8, name="wf_c%d" % a, tag=tag, align_bytes=64)
            nc.vector.tensor_copy(
                out=c[:].rearrange("p (t m e) -> p t m e", t=PACK, e=2),
                in_=wf_raw[:, 2 * KP * a : 2 * KP * (a + 1)].rearrange("p (m t e) -> p t m e", t=PACK, e=2),
            )
            return c

        pages = {}
        wf_raw = keep.tile([P, 2 * H], U8, name="wf_raw", align_bytes=64)
        nc.sync.dma_start(out=wf_raw[:].bitcast(I32), in_=wf_words[0].bitcast(I32))
        idx2 = load_list(offs2, "idx2")
        load_scale_rows(nc.sync, wf_plane, wf_scales)
        wg2_rows = load_factor(wg2, "wg2")
        tab2_w = load_table_words(tab2_words[0], "tab2_w")
        load_scale_rows(nc.sync, tab2_plane, tab2_scales)
        gain = lists.tile([P, 2, PACK], F32, name="gain")
        nc.sync.dma_start(out=gain[:], in_=gf.rearrange("(a p t) -> p a t", a=2, t=PACK))
        pages[0, 0] = load_page(0, 0)
        idx4 = load_list(offs4, "idx4")

        g2 = [keep.tile([P, PACK, S], F32, name="g2_%d" % a, tag=("g2", "x_second")[a], align_bytes=64) for a in range(2)]
        wg2_turned = turn_factor(wg2_rows)

        def deal_frost_factor(t, bank_pool):
            back = deal_factor(wg2_turned, t, bank_pool)
            for a in range(2):
                nc.scalar.activation(out=g2[a][:, t, :], in_=back[:], func=ACT.Copy, scale=gain[:, a, t : t + 1])

        deal_frost_factor(0, psum)
        wf_s = keep.tile([P, H], U8, name="wf_s", align_bytes=64)
        nc.vector.tensor_copy(
            out=wf_s[:].rearrange("p (b t m) -> p b t m", t=PACK, m=P),
            in_=wf_plane[:].rearrange("p (b m t) -> p b t m", t=PACK, m=P),
        )
        wf_c = [deal_wf_words(0, "wf_c0")]
        v2_c = gather(tab2_w, idx2, U32, "v2_c")
        v2_s = gather(tab2_plane, idx2, U8, "v2_s")
        wf_c.append(deal_wf_words(1, "tab2_plane"))

        def frost_features(a, t):
            acc = (side if (a, t) == (0, 0) else psum).tile([P, NB], F32, name="acc", tag="acc")
            nc.tensor.matmul_mx(
                out=acc[:],
                lhsT=wf_c[a][:, 2 * P * t : 2 * P * (t + 1)].bitcast(FP4X4),
                lhsT_scale=wf_s[:, KP * a + P * t : KP * a + P * (t + 1)],
                rhs=v2_c[:].bitcast(FP8X4),
                rhs_scale=v2_s[:],
                start=True,
                stop=True,
            )
            h = feat.tile([P, S], F32, name="h", tag="h", align_bytes=64)
            nc.scalar.activation(out=h[:], in_=acc[:], func=ACT.Gelu_apprx_tanh)
            return h

        h2 = {(0, 0): frost_features(0, 0)}
        for t in range(1, PACK):
            deal_frost_factor(t, side)
            h2[0, t] = frost_features(0, t)
        for t in range(PACK):
            h2[1, t] = frost_features(1, t)

        def frost(a, t):
            nc.vector.tensor_tensor(pages[a, t][:].indirect(idx4[:]), h2[a, t][:], g2[a][:, t, :], MULT)

        v_c, wa_q = [], {}
        frost(0, 0)
        pages[0, 1] = load_page(0, 1)
        frost(0, 1)
        pages[0, 2] = load_page(0, 2)
        frost(0, 2)
        idx = load_list(offs, "idx")
        v_c.append(gather(load_table_words(tab_words[0], "tab_w0"), idx, U32, "v_c0"))
        pages[0, 3] = load_page(0, 3)
        frost(0, 3)
        wg1_turned = turn_factor(load_factor(wg1, "wg1"))
        g1 = keep.tile([P, PACK, S], F32, name="g1", align_bytes=64)
        for t in range(PACK):
            nc.scalar.copy(out=g1[:, t, :], in_=deal_factor(wg1_turned, t, side)[:])
        wa_q[0, 0] = quantise_weight(load_rows(wa, 0, 0, "wa00"), "wa00", "q00")
        pages[1, 0] = load_page(1, 0)
        frost(1, 0)
        wa_q[1, 0] = quantise_weight(load_rows(wa, 1, 0, "wa10"), "wa10", "q01")
        pages[1, 1] = load_page(1, 1)
        frost(1, 1)
        v_c.append(gather(load_table_words(tab_words[1], "tab_w1"), idx, U32, "v_c1"))
        pages[1, 2] = load_page(1, 2)
        frost(1, 2)
        load_scale_rows(nc.sync, tab_plane, tab_scales)
        v_s = gather(tab_plane, idx, U8, "v_s")
        pages[1, 3] = load_page(1, 3)
        frost(1, 3)

        def weather(a, t, pool=feat, tag="h"):
            acc = psum.tile([P, NB], F32, name="acc", tag="acc")
            for g in range(2):
                codes, scales = wa_q[g, a]
                nc.tensor.matmul_mx(
                    out=acc[:],
                    lhsT=codes[:, P * t : P * (t + 1)].bitcast(FP8X4),
                    lhsT_scale=scales[:, P * t : P * (t + 1)],
                    rhs=v_c[g][:].bitcast(FP8X4),
                    rhs_scale=v_s[4 * g :, :],
                    start=(g == 0),
                    stop=(g == 1),
                )
            h = pool.tile([P, S], F32, name="h", tag=tag, align_bytes=64)
            nc.scalar.activation(out=h[:], in_=acc[:], func=ACT.Abs)
            nc.vector.tensor_tensor(pages[a, t][:].indirect(idx3[:]), h[:], g1[:, t, :], MULT)

        wa_q[0, 1] = quantise_weight(load_rows(wa, 0, 1, "wa01"), "wa01", "q10")
        idx3 = load_list(offs3, "idx3")
        for t in range(PACK - 1):
            weather(0, t)
        wa_q[1, 1] = quantise_weight(load_rows(wa, 1, 1, "wa11", keep, "z_first"), "wa11", "q11")
        weather(0, PACK - 1, keep, "z_first")
        for t in range(PACK):
            weather(1, t)
        ws_q = {}
        for a in range(2):
            for g in range(2):
                ws_q[g, a] = quantise_weight(load_rows(ws, g, a, "ws%d%d" % (g, a)), "ws%d%d" % (g, a), "ws%d%d" % (g, a))

        load_scale_rows(nc.sync, wr_plane, wr_scales)
        wr_raw = stream.tile([P, 2, H], I32, name="wr_raw", tag="big", align_bytes=64)
        nc.sync.dma_start(out=wr_raw[:], in_=wr_words.rearrange("g p c i -> p g (c i)").bitcast(I32))
        wr_c = keep.tile([P, 2 * H], I32, name="wr_c", align_bytes=64)
        wr_s = keep.tile([P, H], U8, name="wr_s", align_bytes=64)
        nc.vector.tensor_copy(
            out=wr_c[:].rearrange("p (b t m i) -> p b m t i", t=PACK, m=32, i=4),
            in_=wr_raw[:].rearrange("p g c -> p (g c)").rearrange("p (b m i t) -> p b m t i", t=PACK, m=32, i=4),
        )
        nc.vector.tensor_copy(
            out=wr_s[:].rearrange("p (b t m) -> p b t m", t=PACK, m=P),
            in_=wr_plane[:].rearrange("p (b m t) -> p b t m", t=PACK, m=P),
        )

        idx5 = load_list(offs5, "idx5")
        exs = {}
        for half in range(2):
            for a in range(2):
                exs[a, half] = load_rows(ex, a, half, "ex%d%d" % (a, half))
        xs, zs, z_q = {}, {}, {}

        x_tag = ("g1", "x_second", "z_first", "g2")
        z_tag = ("z_first", "g2", "g1", "x_second")

        def read_slots(c):
            both = keep.tile([P, 2, PACK, CH], F32, name="x%d" % c, tag=x_tag[c], align_bytes=64)
            zs[c] = keep.tile([P, 2, PACK * CH], BF16, name="z%d" % c, tag=z_tag[c], align_bytes=64)
            cols = slice(CH * (c % 2), CH * (c % 2 + 1))
            for a in range(2):
                x = both[:, a]
                zf = flat.tile([P, PACK, CH], BF16, name="zf", tag="zf")
                for t in range(PACK):
                    nc.vector.tensor_copy(x[:, t, :], pages[a, t][:].indirect(idx5[:, 16 * c : 16 * (c + 1)]))
                    if t % 2 == 1:
                        nc.gpsimd.tensor_tensor(
                            zf[:, t - 1 : t + 1, :], x[:, t - 1 : t + 1, :], exs[a, c // 2][:, t - 1 : t + 1, cols], MULT
                        )
                nc.scalar.copy(
                    out=zs[c][:, a, :].rearrange("p (c i t) -> p c t i", i=4, t=PACK),
                    in_=zf[:].rearrange("p t (c i) -> p c t i", i=4),
                )
                xs[c, a] = x

        def quantise_z(c):
            codes = keep.tile([P, NB], U32, name="zc%d" % c, tag="q%d%dc" % (c // 2, c % 2), align_bytes=64)
            scales = keep.tile([P, NB], U8, name="zs%d" % c, tag="q%d%ds" % (c // 2, c % 2), align_bytes=64)
            nc.vector.quantize_mx(out=codes[:].bitcast(FP8X4), scales=scales[:], in_=zs[c][:].rearrange("p a w -> p (a w)"))
            z_q[c] = codes, scales

        def scores(c):
            zc, zsc = z_q[c]
            late = []
            for u in range(4):
                a, t0 = u // 2, 2 * (u % 2)
                y = psum.tile([P, 2, CH], F32, name="acc", tag="acc")
                rest = (side if u == 3 else psum).tile([P, 2, CH], F32, name="acc", tag="acc")
                for i in range(2):
                    for g in range(2):
                        codes, scales = ws_q[g, a]
                        col = P * (t0 + i)
                        nc.tensor.matmul_mx(
                            out=y[:, i, :],
                            lhsT=codes[:, col : col + P].bitcast(FP8X4),
                            lhsT_scale=scales[:, col : col + P],
                            rhs=zc[:, CH * g : CH * (g + 1)].bitcast(FP8X4),
                            rhs_scale=zsc[:, CH * g : CH * (g + 1)],
                            start=(g == 0),
                            stop=(g == 1),
                        )
                for i in range(2):
                    for g in range(2):
                        col = KP * a + P * (t0 + i)
                        nc.tensor.matmul_mx(
                            out=rest[:, i, :],
                            lhsT=wr_c[:, H * g + col : H * g + col + P].bitcast(FP8X4),
                            lhsT_scale=wr_s[4 * g :, col : col + P],
                            rhs=zc[:, CH * g : CH * (g + 1)].bitcast(FP8X4),
                            rhs_scale=zsc[:, CH * g : CH * (g + 1)],
                            start=(g == 0),
                            stop=(g == 1),
                        )
                o = feat.tile([P, 2, CH], F32, name="o", tag="h", align_bytes=64)
                dst = out.rearrange("(a p t) m -> a p t m", a=2, t=PACK)[a][:, t0 : t0 + 2, CH * c : CH * (c + 1)]
                nc.vector.tensor_tensor(o[:], y[:], xs[c, a][:, t0 : t0 + 2, :], MULT)
                for o2, rest2, dst2 in late:
                    nc.vector.tensor_tensor(o2[:], rest2[:], o2[:], ADD)
                    nc.sync.dma_start(out=dst2, in_=o2[:])
                late = []
                if u < (0,2,2,1)[c]:
                    r = flat.tile([P, 2, CH], F32, name="r", tag="r", bufs=2)
                    nc.scalar.copy(out=r[:], in_=rest[:])
                    nc.gpsimd.tensor_tensor(o[:], r[:], o[:], ADD)
                    nc.sync.dma_start(out=dst, in_=o[:])
                else:
                    late.append((o, rest, dst))
            for o2, rest2, dst2 in late:
                nc.vector.tensor_tensor(o2[:], rest2[:], o2[:], ADD)
                nc.sync.dma_start(out=dst2, in_=o2[:])

        read_slots(0)
        read_slots(1)
        quantise_z(0)
        read_slots(2)
        quantise_z(1)
        scores(0)
        read_slots(3)
        quantise_z(2)
        scores(1)
        quantise_z(3)
        scores(2)
        scores(3)
